import numpy as np
import ml_dtypes


def mxq(x, axis, fmt="e4m3"):
    dtype, down = {"e4m3": (ml_dtypes.float8_e4m3fn, 7), "e5m2": (ml_dtypes.float8_e5m2, 14)}[fmt]
    v = np.moveaxis(np.asarray(x, np.float32).astype(ml_dtypes.bfloat16).astype(np.float64), axis, -1)
    blocks = v.reshape(v.shape[:-1] + (-1, 32))
    amax = np.abs(blocks).max(-1, keepdims=True)
    byte = np.maximum(np.where(amax > 0, np.frexp(amax)[1] - 1 + 127, 0) - down, 1)
    scale = np.exp2(byte - 127.0)
    codes = (blocks / scale).astype(np.float32).astype(dtype).astype(np.float64)
    return np.moveaxis((codes * scale).reshape(v.shape), -1, axis)


WIDE = False


def mx_kscale(k):
    if not WIDE:
        return np.ones(k)
    levels = np.array([10, -10, 5, -5, 0])
    if k % 512:
        return np.exp2(np.random.permutation(np.resize(levels, k // 32))).repeat(32)
    a = np.empty((k // 512, 16))
    for p in range(k // 512):
        a[p, :8] = np.random.permutation(np.resize(levels, 8))
        for g in range(8):
            far = levels[np.abs(levels - a[p, g]) >= 10]
            a[p, g + 8] = far[np.random.randint(len(far))]
    return np.exp2(a.ravel()).repeat(32)


def f64(x):
    return np.asarray(x).astype(np.float64)


def striped(idx):
    return np.tile(idx.reshape(-1, 16).T, (8, 1)).astype(np.uint16)


def unstriped(offs):
    return offs[:16].T.reshape(-1).astype(np.int64)


def striped8(idx):
    return np.concatenate([x.reshape(-1, 16).T for x in idx]).astype(np.uint16)


def runs(offs, k):
    lists = np.stack([offs[16 * r : 16 * r + 16].T.reshape(-1) for r in range(8)]).astype(np.int64)
    return lists[np.arange(k) % 512 // 64]


def pack_weight(w):
    k, n = w.shape
    w = f64(np.asarray(w, np.float32).astype(ml_dtypes.bfloat16)).reshape(k // 32, 32, n)
    amax = np.abs(w).max(1)
    byte = np.clip(np.where(amax > 0, np.frexp(amax)[1] - 1 + 127 - 7, 1), 1, 254)
    scaled = (w * np.exp2(127.0 - byte)[:, None, :]).reshape(k, n).astype(np.float32)
    words = np.ascontiguousarray(scaled.reshape(k // 512, 128, 4, n).transpose(0, 1, 3, 2)).astype(ml_dtypes.float8_e4m3fn).view(np.uint8)
    return words, np.ascontiguousarray(byte.astype(np.uint8).reshape(k // 512, 16, n))


def unpack_weight(words, scales):
    g, p, n, _ = words.shape
    vals = np.ascontiguousarray(words).view(ml_dtypes.float8_e4m3fn).astype(np.float64) * np.repeat(np.exp2(scales.astype(np.float64) - 127.0), 8, axis=1)[..., None]
    return vals.transpose(0, 1, 3, 2).reshape(g * 512, n)


def sigmoid(v):
    return 1.0 / (1.0 + np.exp(-np.maximum(v, -700.0)))


K, T, S, V, N, U, H = 512, 2048, 512, 1024, 512, 1024, 512


def setup_inputs():
    n = np.random.standard_normal
    s = mx_kscale(K)[:, None]
    u = mx_kscale(H)
    packed_xT = pack_weight(n((K, T)) * s)
    return {
        "x_words": packed_xT[0],
        "x_scales": packed_xT[1],
        "w1": (n((K, H)) / np.sqrt(K) / s).astype(np.float32),
        "grid": n((H, U)).astype(np.float32),
        "gn": (np.random.uniform(0.5, 1.5, (H, 1)) * u[:, None]).astype(np.float32),
        "w2": (n((H, N)) / np.sqrt(H) / u[:, None]).astype(np.float32),
        "res": (2 * n((N, V))).astype(np.float32),
        "offs": striped(np.random.permutation(T)[:S]),
        "cell": striped8(np.stack([np.random.permutation(U)[:S] for _ in range(8)])),
        "look": striped8(np.stack([np.random.permutation(U) for _ in range(8)])),
    }


def reference(x_words, x_scales, w1, grid, gn, w2, res, offs, cell, look):
    xq = unpack_weight(x_words, x_scales)[:, unstriped(offs)]
    p = np.clip(sigmoid(mxq(f64(w1), 0, "e4m3").T @ xq), 0.1, 0.9)
    nw = np.clip(f64(grid)[np.arange(H)[:, None], runs(cell, H)] + np.log(p / (-1.0 * p + 1)), -2.0, 2.0)
    gd = f64(grid).copy()
    gd[np.arange(H)[:, None], runs(cell, H)] = nw
    z = f64(gn) * (gd[np.arange(H)[:, None], runs(look, H)])
    return f64(res) + (mxq(f64(w2), 0, "e4m3").T @ mxq(z, 0, "e4m3"))

@@ -1,0 +1,197 @@
+from contextlib import ExitStack
+
+import concourse.mybir as mybir
+
+K, T, S, V, N, U, H = 512, 2048, 512, 1024, 512, 1024, 512
+FLOPS = 2 * K * H * S + 2 * H * N * V
+
+F32 = mybir.dt.float32
+BF16 = mybir.dt.bfloat16
+I32 = mybir.dt.int32
+U32 = mybir.dt.uint32
+U16 = mybir.dt.uint16
+U8 = mybir.dt.uint8
+FP8X4 = mybir.dt.float8_e4m3fn_x4
+ALU = mybir.AluOpType
+ACT = mybir.ActivationFunctionType
+
+P = 128
+PACK = 4
+GROUP = 16
+CHUNK = 256
+LOGIT_MAX = 2.1972245773362196
+ODDS_MAX = 2.0
+
+
+def tile_picked_occread_none_p_kernel(tc, x_words, x_scales, w1, grid, gn, w2, res, offs, cell, look, out):
+    nc = tc.nc
+    with ExitStack() as ctx:
+        keep = ctx.enter_context(tc.tile_pool(name="keep", bufs=1))
+        ring = ctx.enter_context(tc.tile_pool(name="ring", bufs=2))
+        psum = ctx.enter_context(tc.psum_pool(name="psum", bufs=1))
+
+        offs_sb = keep.tile([P, S // GROUP], U16, name="offs_sb")
+        cell_sb = keep.tile([P, S // GROUP], U16, name="cell_sb")
+        look_sb = keep.tile([P, V // GROUP], U16, name="look_sb")
+        table_words = keep.tile([P, T], I32, name="table_words")
+        table_scales = keep.tile([P, T], U8, name="table_scales")
+        nc.gpsimd.memset(table_scales[:].bitcast(I32), 0)
+
+        half = H // 2
+        w1_raw = [keep.tile([P, PACK, half], F32, name=f"w1_raw{h}") for h in range(2)]
+        w2_raw = keep.tile([P, PACK, N], F32, name="w2_raw")
+        gain = keep.tile([P, PACK], F32, name="gain")
+        grid_sb = [keep.tile([P, U], F32, name=f"grid{t}", tag=f"grid{t}") for t in range(PACK)]
+        res_sb = keep.tile([P, PACK, V], F32, name="res_sb")
+        w1_rows = w1.rearrange("(p j) c -> p j c", j=PACK)
+        grid_rows = grid.rearrange("(p t) u -> p t u", t=PACK)
+        res_rows = res.rearrange("(p c) v -> p c v", c=PACK)
+        out_rows = out.rearrange("(p c) v -> p c v", c=PACK)
+        nc.sync.dma_start(offs_sb[:], offs)
+        nc.sync.dma_start(cell_sb[:], cell)
+        nc.sync.dma_start(look_sb[:], look)
+        nc.sync.dma_start(out=gain[:], in_=gn.rearrange("(p t) o -> p (t o)", t=PACK))
+        words_hbm = x_words[0].rearrange("p n t -> p (n t)").bitcast(I32)
+        for q in range(4):
+            cols = slice(q * T // 4, (q + 1) * T // 4)
+            nc.sync.dma_start(out=table_words[:, cols], in_=words_hbm[:, cols])
+        for q in range(4):
+            nc.sync.dma_start(out=table_scales[32 * q : 32 * q + 4, :].bitcast(I32), in_=x_scales[0, 4 * q : 4 * q + 4, :].bitcast(I32))
+        for h in range(2):
+            nc.sync.dma_start(out=w1_raw[h][:], in_=w1_rows[:, :, h * half : (h + 1) * half])
+        for t in range(PACK):
+            nc.sync.dma_start(out=grid_sb[t][:], in_=grid_rows[:, t, :])
+        for c in range(PACK):
+            nc.sync.dma_start(out=res_sb[:, c, :], in_=res_rows[:, c, :])
+        nc.sync.dma_start(out=w2_raw[:], in_=w2.rearrange("(p j) c -> p j c", j=PACK))
+
+        one = keep.tile([P, 1], F32, name="one")
+        nc.gpsimd.memset(one[:], 1.0)
+        biases = []
+        for i, value in enumerate((LOGIT_MAX, 2 * LOGIT_MAX, ODDS_MAX + LOGIT_MAX, 2 * ODDS_MAX, ODDS_MAX)):
+            b = keep.tile([P, 1], F32, name=f"bias{i}")
+            nc.scalar.activation(out=b[:], in_=one[:], func=ACT.Relu, scale=value)
+            biases.append(b)
+        floor = keep.tile([P, S], F32, name="floor")
+        nc.gpsimd.memset(floor[:], -ODDS_MAX)
+
+        picked_scales = keep.tile([P, S], U8, name="picked_scales", align_bytes=64)
+        picked_words = keep.tile([P, S], U32, name="picked_words", align_bytes=64)
+        w1_bf = keep.tile([P, PACK * H], BF16, name="w1_bf", align_bytes=64)
+        w1_codes = keep.tile([P, H], U32, name="w1_codes", align_bytes=64)
+        w1_scales = keep.tile([P, H], U8, name="w1_scales", align_bytes=64)
+        w2_bf = keep.tile([P, PACK * N], BF16, name="w2_bf", align_bytes=64)
+        w2_codes = keep.tile([P, N], U32, name="w2_codes", align_bytes=64)
+        w2_scales = keep.tile([P, N], U8, name="w2_scales", align_bytes=64)
+
+        w1_dealt = w1_bf[:].rearrange("p (t m j) -> p m j t", t=PACK, j=PACK)
+        nc.vector.tensor_copy(out=picked_words[:], in_=table_words[:].bitcast(U32).indirect(offs_sb[:]))
+        nc.vector.tensor_copy(out=picked_scales[:], in_=table_scales[:].indirect(offs_sb[:]))
+        raw = [w1_raw[h][:].rearrange("p j (m t) -> p m j t", t=PACK) for h in range(2)]
+        nc.scalar.copy(out=w1_dealt[:, 0:64], in_=raw[0])
+        nc.vector.tensor_copy(out=w1_dealt[:, 64:108], in_=raw[1][:, 0:44])
+        nc.scalar.copy(out=w1_dealt[:, 108:128], in_=raw[1][:, 44:64])
+        nc.vector.quantize_mx(out=w1_codes[:, 0:P].bitcast(FP8X4), scales=w1_scales[:, 0:P], in_=w1_bf[:, 0 : PACK * P])
+        nc.vector.quantize_mx(out=w1_codes[:, P : 2 * P].bitcast(FP8X4), scales=w1_scales[:, P : 2 * P], in_=w1_bf[:, PACK * P : 2 * PACK * P])
+        nc.vector.quantize_mx(out=w1_codes[:, 2 * P :].bitcast(FP8X4), scales=w1_scales[:, 2 * P :], in_=w1_bf[:, 2 * PACK * P :])
+
+        shifted = []
+        summed = []
+        lifted = []
+        scaled = []
+
+        def project(t):
+            u = psum.tile([P, S], F32, name=f"u{t}")
+            cols = slice(t * P, (t + 1) * P)
+            nc.tensor.matmul_mx(out=u[:], lhsT=w1_codes[:, cols].bitcast(FP8X4), lhsT_scale=w1_scales[:, cols],
+                                rhs=picked_words[:].bitcast(FP8X4), rhs_scale=picked_scales[:], start=True, stop=True)
+            if t == 0:
+                b = keep.tile([P, S], F32, name="b0")
+                nc.vector.tensor_scalar(out=b[:], in0=u[:], scalar1=-LOGIT_MAX, scalar2=LOGIT_MAX, op0=ALU.max, op1=ALU.min)
+                shifted.append(b)
+                return
+            a = keep.tile([P, S], F32, name="a", tag="a")
+            nc.scalar.activation(out=a[:], in_=u[:], func=ACT.Relu, bias=biases[0][:], scale=-1.0)
+            b = keep.tile([P, S], F32, name=f"b{t}")
+            nc.scalar.activation(out=b[:], in_=a[:], func=ACT.Relu, bias=biases[1][:], scale=-1.0)
+            shifted.append(b)
+
+        def fetch(t):
+            s = keep.tile([P, S], F32, name=f"s{t}")
+            nc.vector.tensor_tensor(s[:], grid_sb[t][:].indirect(cell_sb[:]), shifted[t][:], ALU.add)
+            a = keep.tile([P, S], F32, name="a", tag="a")
+            nc.scalar.activation(out=a[:], in_=s[:], func=ACT.Relu, bias=biases[2 if t else 4][:], scale=-1.0)
+            b = keep.tile([P, S], F32, name=f"b2{t}")
+            nc.scalar.activation(out=b[:], in_=a[:], func=ACT.Relu, bias=biases[3][:], scale=-1.0)
+            lifted.append(b)
+
+        def put(t):
+            nc.vector.tensor_tensor(grid_sb[t][:].indirect(cell_sb[:]), lifted[t][:], floor[:], ALU.add)
+
+        def weigh(t):
+            g = keep.tile([P, U], F32, name=f"scaled{t}")
+            nc.scalar.activation(out=g[:], in_=grid_sb[t][:], func=ACT.Copy, scale=gain_late[:, t : t + 1])
+            scaled.append(g)
+
+        project(0)
+        project(1)
+        fetch(0)
+        project(2)
+        fetch(1)
+        project(3)
+        put(0)
+        fetch(2)
+        put(1)
+        fetch(3)
+        put(2)
+        put(3)
+        gain_late = keep.tile([P, PACK], F32, name="gain_late", tag="a")
+        nc.scalar.copy(out=gain_late[:], in_=gain[:])
+        weigh(0)
+        weigh(1)
+        nc.scalar.copy(out=w2_bf[:].rearrange("p (t m j) -> p m j t", t=PACK, j=PACK), in_=w2_raw[:].rearrange("p j (m t) -> p m j t", t=PACK))
+        weigh(2)
+        weigh(3)
+        nc.vector.quantize_mx(out=w2_codes[:].bitcast(FP8X4), scales=w2_scales[:], in_=w2_bf[:])
+
+        chunks = V // CHUNK
+        woven = []
+        banks = []
+
+        def read(q):
+            planes = keep.tile([P, PACK, CHUNK], BF16, name=f"planes{q}", tag="grid3" if q % 2 else "planes")
+            places = look_sb[:, q * CHUNK // GROUP : (q + 1) * CHUNK // GROUP]
+            for t in range(PACK):
+                nc.vector.tensor_copy(out=planes[:, t, :], in_=scaled[t][:].indirect(places))
+            z = keep.tile([P, PACK * CHUNK], BF16, name=f"z{q}", align_bytes=64)
+            nc.scalar.copy(out=z[:].rearrange("p (c i t) -> p c t i", i=4, t=PACK), in_=planes[:].rearrange("p t (c i) -> p c t i", i=4))
+            woven.append(z)
+
+        def multiply(q):
+            codes = keep.tile([P, CHUNK], U32, name=f"z_codes{q}", align_bytes=64)
+            scales = keep.tile([P, CHUNK], U8, name=f"z_scales{q}", align_bytes=64)
+            nc.vector.quantize_mx(out=codes[:].bitcast(FP8X4), scales=scales[:], in_=woven[q][:])
+            pair = []
+            for b in range(2):
+                y = psum.tile([P, 2, CHUNK], F32, name=f"y{q % 2}{b}")
+                for e in range(2):
+                    cols = slice((2 * b + e) * P, (2 * b + e + 1) * P)
+                    nc.tensor.matmul_mx(out=y[:, e, :], lhsT=w2_codes[:, cols].bitcast(FP8X4), lhsT_scale=w2_scales[:, cols],
+                                        rhs=codes[:].bitcast(FP8X4), rhs_scale=scales[:], start=True, stop=True)
+                pair.append(y)
+            banks.append(pair)
+
+        def finish(q):
+            cols = slice(q * CHUNK, (q + 1) * CHUNK)
+            for b in range(2):
+                o = keep.tile([P, 2, CHUNK], F32, name=f"o{q}{b}")
+                nc.vector.tensor_tensor(o[:], banks[q][b][:], res_sb[:, 2 * b : 2 * b + 2, cols], ALU.add)
+                nc.sync.dma_start(out=out_rows[:, 2 * b : 2 * b + 2, cols], in_=o[:])
+
+        for q in range(chunks + 2):
+            if q < chunks:
+                read(q)
+            if 1 <= q <= chunks:
+                multiply(q - 1)
+            if q >= 2:
+                finish(q - 2)

@@ -45,22 +45,20 @@ def tile_picked_occread_none_p_kernel(tc, x_words, x_scales, w1, grid, gn, w2, r
         res_sb = keep.tile([P, PACK, V], F32, name="res_sb")
         w1_rows = w1.rearrange("(p j) c -> p j c", j=PACK)
         grid_rows = grid.rearrange("(p t) u -> p t u", t=PACK)
-        res_rows = res.rearrange("(p c) v -> p c v", c=PACK)
-        out_rows = out.rearrange("(p c) v -> p c v", c=PACK)
+        res_rows = res.rearrange("(c p) v -> p c v", c=PACK)
+        out_rows = out.rearrange("(c p) v -> p c v", c=PACK)
+        landed_scales = keep.tile([P, T // 4], I32, name="landed_scales")
         nc.sync.dma_start(offs_sb[:], offs)
-        nc.sync.dma_start(cell_sb[:], cell)
-        nc.sync.dma_start(look_sb[:], look)
-        nc.sync.dma_start(out=gain[:], in_=gn.rearrange("(p t) o -> p (t o)", t=PACK))
-        words_hbm = x_words[0].rearrange("p n t -> p (n t)").bitcast(I32)
         for q in range(4):
-            cols = slice(q * T // 4, (q + 1) * T // 4)
-            nc.sync.dma_start(out=table_words[:, cols], in_=words_hbm[:, cols])
-        for q in range(4):
-            nc.sync.dma_start(out=table_scales[32 * q : 32 * q + 4, :].bitcast(I32), in_=x_scales[0, 4 * q : 4 * q + 4, :].bitcast(I32))
+            nc.sync.dma_start(out=landed_scales[32 * q : 32 * q + 4, :], in_=x_scales[0, 4 * q : 4 * q + 4, :].bitcast(I32))
         for h in range(2):
             nc.sync.dma_start(out=w1_raw[h][:], in_=w1_rows[:, :, h * half : (h + 1) * half])
+        nc.sync.dma_start(out=table_words[:], in_=x_words[0].rearrange("p n t -> p (n t)").bitcast(I32))
+        nc.sync.dma_start(cell_sb[:], cell)
         for t in range(PACK):
             nc.sync.dma_start(out=grid_sb[t][:], in_=grid_rows[:, t, :])
+        nc.sync.dma_start(look_sb[:], look)
+        nc.sync.dma_start(out=gain[:], in_=gn.rearrange("(p t) o -> p (t o)", t=PACK))
         for c in range(PACK):
             nc.sync.dma_start(out=res_sb[:, c, :], in_=res_rows[:, c, :])
         nc.sync.dma_start(out=w2_raw[:], in_=w2.rearrange("(p j) c -> p j c", j=PACK))
@@ -84,32 +82,42 @@ def tile_picked_occread_none_p_kernel(tc, x_words, x_scales, w1, grid, gn, w2, r
         w2_codes = keep.tile([P, N], U32, name="w2_codes", align_bytes=64)
         w2_scales = keep.tile([P, N], U8, name="w2_scales", align_bytes=64)
 
-        w1_dealt = w1_bf[:].rearrange("p (t m j) -> p m j t", t=PACK, j=PACK)
-        nc.vector.tensor_copy(out=picked_words[:], in_=table_words[:].bitcast(U32).indirect(offs_sb[:]))
-        nc.vector.tensor_copy(out=picked_scales[:], in_=table_scales[:].indirect(offs_sb[:]))
-        raw = [w1_raw[h][:].rearrange("p j (m t) -> p m j t", t=PACK) for h in range(2)]
-        nc.scalar.copy(out=w1_dealt[:, 0:64], in_=raw[0])
-        nc.vector.tensor_copy(out=w1_dealt[:, 64:108], in_=raw[1][:, 0:44])
-        nc.scalar.copy(out=w1_dealt[:, 108:128], in_=raw[1][:, 44:64])
-        nc.vector.quantize_mx(out=w1_codes[:, 0:P].bitcast(FP8X4), scales=w1_scales[:, 0:P], in_=w1_bf[:, 0 : PACK * P])
-        nc.vector.quantize_mx(out=w1_codes[:, P : 2 * P].bitcast(FP8X4), scales=w1_scales[:, P : 2 * P], in_=w1_bf[:, PACK * P : 2 * PACK * P])
-        nc.vector.quantize_mx(out=w1_codes[:, 2 * P :].bitcast(FP8X4), scales=w1_scales[:, 2 * P :], in_=w1_bf[:, 2 * PACK * P :])
+        w1_dealt = w1_bf[:].rearrange("p (t m j) -> p t m j", t=PACK, j=PACK)
+        raw = [w1_raw[h][:].rearrange("p j (m t) -> p t m j", t=PACK) for h in range(2)]
+        for q in range(4):
+            rows = slice(32 * q, 32 * q + 4)
+            nc.vector.tensor_copy(out=table_scales[rows, :].bitcast(I32), in_=landed_scales[rows, :])
+        for h in range(2):
+            nc.vector.tensor_copy(out=w1_dealt[:, :, 64 * h : 64 * h + 32], in_=raw[h][:, :, 0:32])
+            nc.scalar.copy(out=w1_dealt[:, :, 64 * h + 32 : 64 * h + 64], in_=raw[h][:, :, 32:64])
+            if h == 0:
+                nc.vector.tensor_copy(out=picked_scales[:], in_=table_scales[:].indirect(offs_sb[:]))
+        nc.vector.quantize_mx(out=w1_codes[:].bitcast(FP8X4), scales=w1_scales[:], in_=w1_bf[:])
+        for h in range(2):
+            nc.vector.tensor_copy(out=picked_words[:, h * 256 : (h + 1) * 256], in_=table_words[:].bitcast(U32).indirect(offs_sb[:, h * 16 : (h + 1) * 16]))
 
         shifted = []
         summed = []
         lifted = []
         scaled = []
 
-        def project(t):
-            u = psum.tile([P, S], F32, name=f"u{t}")
+        def product(u, t, rays):
             cols = slice(t * P, (t + 1) * P)
             nc.tensor.matmul_mx(out=u[:], lhsT=w1_codes[:, cols].bitcast(FP8X4), lhsT_scale=w1_scales[:, cols],
-                                rhs=picked_words[:].bitcast(FP8X4), rhs_scale=picked_scales[:], start=True, stop=True)
+                                rhs=picked_words[:, rays].bitcast(FP8X4), rhs_scale=picked_scales[:, rays], start=True, stop=True)
+
+        def project(t):
             if t == 0:
                 b = keep.tile([P, S], F32, name="b0")
-                nc.vector.tensor_scalar(out=b[:], in0=u[:], scalar1=-LOGIT_MAX, scalar2=LOGIT_MAX, op0=ALU.max, op1=ALU.min)
+                for h in range(2):
+                    rays = slice(h * 256, (h + 1) * 256)
+                    u = psum.tile([P, 256], F32, name=f"u0{h}", tag=f"bank{h}")
+                    product(u, t, rays)
+                    nc.vector.tensor_scalar(out=b[:, rays], in0=u[:], scalar1=-LOGIT_MAX, scalar2=LOGIT_MAX, op0=ALU.max, op1=ALU.min)
                 shifted.append(b)
                 return
+            u = psum.tile([P, S], F32, name=f"u{t}", tag=f"bank{t + 1}")
+            product(u, t, slice(0, S))
             a = keep.tile([P, S], F32, name="a", tag="a")
             nc.scalar.activation(out=a[:], in_=u[:], func=ACT.Relu, bias=biases[0][:], scale=-1.0)
             b = keep.tile([P, S], F32, name=f"b{t}")
@@ -149,7 +157,7 @@ def tile_picked_occread_none_p_kernel(tc, x_words, x_scales, w1, grid, gn, w2, r
         nc.scalar.copy(out=gain_late[:], in_=gain[:])
         weigh(0)
         weigh(1)
-        nc.scalar.copy(out=w2_bf[:].rearrange("p (t m j) -> p m j t", t=PACK, j=PACK), in_=w2_raw[:].rearrange("p j (m t) -> p m j t", t=PACK))
+        nc.scalar.copy(out=w2_bf[:].rearrange("p (c i t) -> p c t i", i=4, t=PACK), in_=w2_raw[:].rearrange("p t (c i) -> p c t i", i=4))
         weigh(2)
         weigh(3)
         nc.vector.quantize_mx(out=w2_codes[:].bitcast(FP8X4), scales=w2_scales[:], in_=w2_bf[:])
@@ -173,7 +181,7 @@ def tile_picked_occread_none_p_kernel(tc, x_words, x_scales, w1, grid, gn, w2, r
             nc.vector.quantize_mx(out=codes[:].bitcast(FP8X4), scales=scales[:], in_=woven[q][:])
             pair = []
             for b in range(2):
-                y = psum.tile([P, 2, CHUNK], F32, name=f"y{q % 2}{b}")
+                y = psum.tile([P, 2, CHUNK], F32, name=f"y{q}{b}", tag=f"bank{(5 + 2 * q + b) % 8}")
                 for e in range(2):
                     cols = slice((2 * b + e) * P, (2 * b + e + 1) * P)
                     nc.tensor.matmul_mx(out=y[:, e, :], lhsT=w2_codes[:, cols].bitcast(FP8X4), lhsT_scale=w2_scales[:, cols],

@@ -19,6 +19,7 @@ P = 128
 PACK = 4
 GROUP = 16
 CHUNK = 256
+POOL_CHUNKS = 2
 LOGIT_MAX = 2.1972245773362196
 ODDS_MAX = 2.0
 
@@ -179,27 +180,38 @@ def tile_picked_occread_none_p_kernel(tc, x_words, x_scales, w1, grid, gn, w2, r
             codes = keep.tile([P, CHUNK], U32, name=f"z_codes{q}", align_bytes=64)
             scales = keep.tile([P, CHUNK], U8, name=f"z_scales{q}", align_bytes=64)
             nc.vector.quantize_mx(out=codes[:].bitcast(FP8X4), scales=scales[:], in_=woven[q][:])
-            pair = []
-            for b in range(2):
-                y = psum.tile([P, 2, CHUNK], F32, name=f"y{q}{b}", tag=f"bank{(5 + 2 * q + b) % 8}")
-                for e in range(2):
-                    cols = slice((2 * b + e) * P, (2 * b + e + 1) * P)
+            width = 1 if q == chunks - 1 else 2
+            group = []
+            for b in range(PACK // width):
+                y = psum.tile([P, width, CHUNK], F32, name=f"y{q}{b}", tag=f"bank{(2 * q + b) % 8}")
+                for e in range(width):
+                    cols = slice((width * b + e) * P, (width * b + e + 1) * P)
                     nc.tensor.matmul_mx(out=y[:, e, :], lhsT=w2_codes[:, cols].bitcast(FP8X4), lhsT_scale=w2_scales[:, cols],
                                         rhs=codes[:].bitcast(FP8X4), rhs_scale=scales[:], start=True, stop=True)
-                pair.append(y)
-            banks.append(pair)
+                group.append(y)
+            banks.append(group)
 
         def finish(q):
             cols = slice(q * CHUNK, (q + 1) * CHUNK)
-            for b in range(2):
-                o = keep.tile([P, 2, CHUNK], F32, name=f"o{q}{b}")
-                nc.vector.tensor_tensor(o[:], banks[q][b][:], res_sb[:, 2 * b : 2 * b + 2, cols], ALU.add)
-                nc.sync.dma_start(out=out_rows[:, 2 * b : 2 * b + 2, cols], in_=o[:])
+            width = PACK // len(banks[q])
+            for b, y in enumerate(banks[q]):
+                rows = slice(width * b, width * (b + 1))
+                o = keep.tile([P, width, CHUNK], F32, name=f"o{q}{b}")
+                if q < POOL_CHUNKS:
+                    y_sb = keep.tile([P, width, CHUNK], F32, name=f"y_sb{q}{b}")
+                    nc.scalar.copy(out=y_sb[:], in_=y[:])
+                    for e in range(width):
+                        nc.gpsimd.tensor_tensor(o[:, e, :], y_sb[:, e, :], res_sb[:, width * b + e, cols], ALU.add)
+                else:
+                    nc.vector.tensor_tensor(o[:], y[:], res_sb[:, rows, cols], ALU.add)
+                nc.sync.dma_start(out=out_rows[:, rows, cols], in_=o[:])
 
         for q in range(chunks + 2):
             if q < chunks:
                 read(q)
             if 1 <= q <= chunks:
                 multiply(q - 1)
-            if q >= 2:
+                if q - 1 < POOL_CHUNKS:
+                    finish(q - 1)
+            if q - 2 >= POOL_CHUNKS:
                 finish(q - 2)

@@ -19,7 +19,7 @@ P = 128
 PACK = 4
 GROUP = 16
 CHUNK = 256
-POOL_CHUNKS = 2
+POOL_CHUNKS = 0
 LOGIT_MAX = 2.1972245773362196
 ODDS_MAX = 2.0
 
@@ -39,7 +39,7 @@ def tile_picked_occread_none_p_kernel(tc, x_words, x_scales, w1, grid, gn, w2, r
         nc.gpsimd.memset(table_scales[:].bitcast(I32), 0)
 
         half = H // 2
-        w1_raw = [keep.tile([P, PACK, half], F32, name=f"w1_raw{h}") for h in range(2)]
+        w1_raw = keep.tile([P, PACK, H], F32, name="w1_raw")
         w2_raw = keep.tile([P, PACK, N], F32, name="w2_raw")
         gain = keep.tile([P, PACK], F32, name="gain")
         grid_sb = [keep.tile([P, U], F32, name=f"grid{t}", tag=f"grid{t}") for t in range(PACK)]
@@ -52,8 +52,7 @@ def tile_picked_occread_none_p_kernel(tc, x_words, x_scales, w1, grid, gn, w2, r
         nc.sync.dma_start(offs_sb[:], offs)
         for q in range(4):
             nc.sync.dma_start(out=landed_scales[32 * q : 32 * q + 4, :], in_=x_scales[0, 4 * q : 4 * q + 4, :].bitcast(I32))
-        for h in range(2):
-            nc.sync.dma_start(out=w1_raw[h][:], in_=w1_rows[:, :, h * half : (h + 1) * half])
+        nc.sync.dma_start(out=w1_raw[:], in_=w1_rows)
         nc.sync.dma_start(out=table_words[:], in_=x_words[0].rearrange("p n t -> p (n t)").bitcast(I32))
         nc.sync.dma_start(cell_sb[:], cell)
         for t in range(PACK):
@@ -83,16 +82,14 @@ def tile_picked_occread_none_p_kernel(tc, x_words, x_scales, w1, grid, gn, w2, r
         w2_codes = keep.tile([P, N], U32, name="w2_codes", align_bytes=64)
         w2_scales = keep.tile([P, N], U8, name="w2_scales", align_bytes=64)
 
-        w1_dealt = w1_bf[:].rearrange("p (t m j) -> p t m j", t=PACK, j=PACK)
-        raw = [w1_raw[h][:].rearrange("p j (m t) -> p t m j", t=PACK) for h in range(2)]
+        w1_dealt = w1_bf[:].rearrange("p (t m j) -> p m j t", t=PACK, j=PACK)
+        raw = w1_raw[:].rearrange("p j (m t) -> p m j t", t=PACK)
         for q in range(4):
             rows = slice(32 * q, 32 * q + 4)
             nc.vector.tensor_copy(out=table_scales[rows, :].bitcast(I32), in_=landed_scales[rows, :])
-        for h in range(2):
-            nc.vector.tensor_copy(out=w1_dealt[:, :, 64 * h : 64 * h + 32], in_=raw[h][:, :, 0:32])
-            nc.scalar.copy(out=w1_dealt[:, :, 64 * h + 32 : 64 * h + 64], in_=raw[h][:, :, 32:64])
-            if h == 0:
-                nc.vector.tensor_copy(out=picked_scales[:], in_=table_scales[:].indirect(offs_sb[:]))
+        nc.vector.tensor_copy(out=picked_scales[:], in_=table_scales[:].indirect(offs_sb[:]))
+        nc.vector.tensor_copy(out=w1_dealt[:, :84], in_=raw[:, :84])
+        nc.scalar.copy(out=w1_dealt[:, 84:], in_=raw[:, 84:])
         nc.vector.quantize_mx(out=w1_codes[:].bitcast(FP8X4), scales=w1_scales[:], in_=w1_bf[:])
         for h in range(2):
             nc.vector.tensor_copy(out=picked_words[:, h * 256 : (h + 1) * 256], in_=table_words[:].bitcast(U32).indirect(offs_sb[:, h * 16 : (h + 1) * 16]))
@@ -168,7 +165,7 @@ def tile_picked_occread_none_p_kernel(tc, x_words, x_scales, w1, grid, gn, w2, r
         banks = []
 
         def read(q):
-            planes = keep.tile([P, PACK, CHUNK], BF16, name=f"planes{q}", tag="grid3" if q % 2 else "planes")
+            planes = keep.tile([P, PACK, CHUNK], F32, name=f"planes{q}", tag="grid3" if q % 2 else "planes")
             places = look_sb[:, q * CHUNK // GROUP : (q + 1) * CHUNK // GROUP]
             for t in range(PACK):
                 nc.vector.tensor_copy(out=planes[:, t, :], in_=scaled[t][:].indirect(places))

from contextlib import ExitStack

import concourse.mybir as mybir

K, T, S, V, N, U, H = 512, 2048, 512, 1024, 512, 1024, 512
FLOPS = 2 * K * H * S + 2 * H * N * V

F32 = mybir.dt.float32
BF16 = mybir.dt.bfloat16
I32 = mybir.dt.int32
U32 = mybir.dt.uint32
U16 = mybir.dt.uint16
U8 = mybir.dt.uint8
FP8X4 = mybir.dt.float8_e4m3fn_x4
ALU = mybir.AluOpType
ACT = mybir.ActivationFunctionType

P = 128
PACK = 4
GROUP = 16
CHUNK = 256
POOL_CHUNKS = 0
LOGIT_MAX = 2.1972245773362196
ODDS_MAX = 2.0


def tile_picked_occread_none_p_kernel(tc, x_words, x_scales, w1, grid, gn, w2, res, offs, cell, look, out):
    nc = tc.nc
    with ExitStack() as ctx:
        keep = ctx.enter_context(tc.tile_pool(name="keep", bufs=1))
        ring = ctx.enter_context(tc.tile_pool(name="ring", bufs=2))
        psum = ctx.enter_context(tc.psum_pool(name="psum", bufs=1))

        offs_sb = keep.tile([P, S // GROUP], U16, name="offs_sb")
        cell_sb = keep.tile([P, S // GROUP], U16, name="cell_sb")
        look_sb = keep.tile([P, V // GROUP], U16, name="look_sb")
        table_words = keep.tile([P, T], I32, name="table_words")
        table_scales = keep.tile([P, T], U8, name="table_scales")
        nc.gpsimd.memset(table_scales[:].bitcast(I32), 0)

        half = H // 2
        w1_raw = keep.tile([P, PACK, H], F32, name="w1_raw")
        w2_raw = keep.tile([P, PACK, N], F32, name="w2_raw")
        gain = keep.tile([P, PACK], F32, name="gain")
        grid_sb = [keep.tile([P, U], F32, name=f"grid{t}", tag=f"grid{t}") for t in range(PACK)]
        res_sb = keep.tile([P, PACK, V], F32, name="res_sb")
        w1_rows = w1.rearrange("(p j) c -> p j c", j=PACK)
        grid_rows = grid.rearrange("(p t) u -> p t u", t=PACK)
        res_rows = res.rearrange("(c p) v -> p c v", c=PACK)
        out_rows = out.rearrange("(c p) v -> p c v", c=PACK)
        landed_scales = keep.tile([P, T // 4], I32, name="landed_scales")
        nc.sync.dma_start(offs_sb[:], offs)
        for q in range(4):
            nc.sync.dma_start(out=landed_scales[32 * q : 32 * q + 4, :], in_=x_scales[0, 4 * q : 4 * q + 4, :].bitcast(I32))
        nc.sync.dma_start(out=w1_raw[:], in_=w1_rows)
        nc.sync.dma_start(out=table_words[:], in_=x_words[0].rearrange("p n t -> p (n t)").bitcast(I32))
        nc.sync.dma_start(cell_sb[:], cell)
        for t in range(PACK):
            nc.sync.dma_start(out=grid_sb[t][:], in_=grid_rows[:, t, :])
        nc.sync.dma_start(look_sb[:], look)
        nc.sync.dma_start(out=gain[:], in_=gn.rearrange("(p t) o -> p (t o)", t=PACK))
        for c in range(PACK):
            nc.sync.dma_start(out=res_sb[:, c, :], in_=res_rows[:, c, :])
        nc.sync.dma_start(out=w2_raw[:], in_=w2.rearrange("(p j) c -> p j c", j=PACK))

        one = keep.tile([P, 1], F32, name="one")
        nc.gpsimd.memset(one[:], 1.0)
        biases = []
        for i, value in enumerate((LOGIT_MAX, 2 * LOGIT_MAX, ODDS_MAX + LOGIT_MAX, 2 * ODDS_MAX, ODDS_MAX)):
            b = keep.tile([P, 1], F32, name=f"bias{i}")
            nc.scalar.activation(out=b[:], in_=one[:], func=ACT.Relu, scale=value)
            biases.append(b)
        floor = keep.tile([P, S], F32, name="floor")
        nc.gpsimd.memset(floor[:], -ODDS_MAX)

        picked_scales = keep.tile([P, S], U8, name="picked_scales", align_bytes=64)
        picked_words = keep.tile([P, S], U32, name="picked_words", align_bytes=64)
        w1_bf = keep.tile([P, PACK * H], BF16, name="w1_bf", align_bytes=64)
        w1_codes = keep.tile([P, H], U32, name="w1_codes", align_bytes=64)
        w1_scales = keep.tile([P, H], U8, name="w1_scales", align_bytes=64)
        w2_bf = keep.tile([P, PACK * N], BF16, name="w2_bf", align_bytes=64)
        w2_codes = keep.tile([P, N], U32, name="w2_codes", align_bytes=64)
        w2_scales = keep.tile([P, N], U8, name="w2_scales", align_bytes=64)

        w1_dealt = w1_bf[:].rearrange("p (t m j) -> p m j t", t=PACK, j=PACK)
        raw = w1_raw[:].rearrange("p j (m t) -> p m j t", t=PACK)
        for q in range(4):
            rows = slice(32 * q, 32 * q + 4)
            nc.vector.tensor_copy(out=table_scales[rows, :].bitcast(I32), in_=landed_scales[rows, :])
        nc.vector.tensor_copy(out=picked_scales[:], in_=table_scales[:].indirect(offs_sb[:]))
        nc.vector.tensor_copy(out=w1_dealt[:, :84], in_=raw[:, :84])
        nc.scalar.copy(out=w1_dealt[:, 84:], in_=raw[:, 84:])
        nc.vector.quantize_mx(out=w1_codes[:].bitcast(FP8X4), scales=w1_scales[:], in_=w1_bf[:])
        for h in range(2):
            nc.vector.tensor_copy(out=picked_words[:, h * 256 : (h + 1) * 256], in_=table_words[:].bitcast(U32).indirect(offs_sb[:, h * 16 : (h + 1) * 16]))

        shifted = []
        summed = []
        lifted = []
        scaled = []

        def product(u, t, rays):
            cols = slice(t * P, (t + 1) * P)
            nc.tensor.matmul_mx(out=u[:], lhsT=w1_codes[:, cols].bitcast(FP8X4), lhsT_scale=w1_scales[:, cols],
                                rhs=picked_words[:, rays].bitcast(FP8X4), rhs_scale=picked_scales[:, rays], start=True, stop=True)

        def project(t):
            if t == 0:
                b = keep.tile([P, S], F32, name="b0")
                for h in range(2):
                    rays = slice(h * 256, (h + 1) * 256)
                    u = psum.tile([P, 256], F32, name=f"u0{h}", tag=f"bank{h}")
                    product(u, t, rays)
                    nc.vector.tensor_scalar(out=b[:, rays], in0=u[:], scalar1=-LOGIT_MAX, scalar2=LOGIT_MAX, op0=ALU.max, op1=ALU.min)
                shifted.append(b)
                return
            u = psum.tile([P, S], F32, name=f"u{t}", tag=f"bank{t + 1}")
            product(u, t, slice(0, S))
            a = keep.tile([P, S], F32, name="a", tag="a")
            nc.scalar.activation(out=a[:], in_=u[:], func=ACT.Relu, bias=biases[0][:], scale=-1.0)
            b = keep.tile([P, S], F32, name=f"b{t}")
            nc.scalar.activation(out=b[:], in_=a[:], func=ACT.Relu, bias=biases[1][:], scale=-1.0)
            shifted.append(b)

        def fetch(t):
            s = keep.tile([P, S], F32, name=f"s{t}")
            nc.vector.tensor_tensor(s[:], grid_sb[t][:].indirect(cell_sb[:]), shifted[t][:], ALU.add)
            a = keep.tile([P, S], F32, name="a", tag="a")
            nc.scalar.activation(out=a[:], in_=s[:], func=ACT.Relu, bias=biases[2 if t else 4][:], scale=-1.0)
            b = keep.tile([P, S], F32, name=f"b2{t}")
            nc.scalar.activation(out=b[:], in_=a[:], func=ACT.Relu, bias=biases[3][:], scale=-1.0)
            lifted.append(b)

        def put(t):
            nc.vector.tensor_tensor(grid_sb[t][:].indirect(cell_sb[:]), lifted[t][:], floor[:], ALU.add)

        def weigh(t):
            g = keep.tile([P, U], F32, name=f"scaled{t}")
            nc.scalar.activation(out=g[:], in_=grid_sb[t][:], func=ACT.Copy, scale=gain_late[:, t : t + 1])
            scaled.append(g)

        project(0)
        project(1)
        fetch(0)
        project(2)
        fetch(1)
        project(3)
        put(0)
        fetch(2)
        put(1)
        fetch(3)
        put(2)
        put(3)
        gain_late = keep.tile([P, PACK], F32, name="gain_late", tag="a")
        nc.scalar.copy(out=gain_late[:], in_=gain[:])
        weigh(0)
        weigh(1)
        nc.scalar.copy(out=w2_bf[:].rearrange("p (c i t) -> p c t i", i=4, t=PACK), in_=w2_raw[:].rearrange("p t (c i) -> p c t i", i=4))
        weigh(2)
        weigh(3)
        nc.vector.quantize_mx(out=w2_codes[:].bitcast(FP8X4), scales=w2_scales[:], in_=w2_bf[:])

        chunks = V // CHUNK
        woven = []
        banks = []

        def read(q):
            planes = keep.tile([P, PACK, CHUNK], F32, name=f"planes{q}", tag="grid3" if q % 2 else "planes")
            places = look_sb[:, q * CHUNK // GROUP : (q + 1) * CHUNK // GROUP]
            for t in range(PACK):
                nc.vector.tensor_copy(out=planes[:, t, :], in_=scaled[t][:].indirect(places))
            z = keep.tile([P, PACK * CHUNK], BF16, name=f"z{q}", align_bytes=64)
            nc.scalar.copy(out=z[:].rearrange("p (c i t) -> p c t i", i=4, t=PACK), in_=planes[:].rearrange("p t (c i) -> p c t i", i=4))
            woven.append(z)

        def multiply(q):
            codes = keep.tile([P, CHUNK], U32, name=f"z_codes{q}", align_bytes=64)
            scales = keep.tile([P, CHUNK], U8, name=f"z_scales{q}", align_bytes=64)
            nc.vector.quantize_mx(out=codes[:].bitcast(FP8X4), scales=scales[:], in_=woven[q][:])
            width = 1 if q == chunks - 1 else 2
            group = []
            for b in range(PACK // width):
                y = psum.tile([P, width, CHUNK], F32, name=f"y{q}{b}", tag=f"bank{(2 * q + b) % 8}")
                for e in range(width):
                    cols = slice((width * b + e) * P, (width * b + e + 1) * P)
                    nc.tensor.matmul_mx(out=y[:, e, :], lhsT=w2_codes[:, cols].bitcast(FP8X4), lhsT_scale=w2_scales[:, cols],
                                        rhs=codes[:].bitcast(FP8X4), rhs_scale=scales[:], start=True, stop=True)
                group.append(y)
            banks.append(group)

        def finish(q):
            cols = slice(q * CHUNK, (q + 1) * CHUNK)
            width = PACK // len(banks[q])
            for b, y in enumerate(banks[q]):
                rows = slice(width * b, width * (b + 1))
                o = keep.tile([P, width, CHUNK], F32, name=f"o{q}{b}")
                if q < POOL_CHUNKS:
                    y_sb = keep.tile([P, width, CHUNK], F32, name=f"y_sb{q}{b}")
                    nc.scalar.copy(out=y_sb[:], in_=y[:])
                    for e in range(width):
                        nc.gpsimd.tensor_tensor(o[:, e, :], y_sb[:, e, :], res_sb[:, width * b + e, cols], ALU.add)
                else:
                    nc.vector.tensor_tensor(o[:], y[:], res_sb[:, rows, cols], ALU.add)
                nc.sync.dma_start(out=out_rows[:, rows, cols], in_=o[:])

        for q in range(chunks + 2):
            if q < chunks:
                read(q)
            if 1 <= q <= chunks:
                multiply(q - 1)
                if q - 1 < POOL_CHUNKS:
                    finish(q - 1)
            if q - 2 >= POOL_CHUNKS:
                finish(q - 2)
